import numpy as np
import ml_dtypes


def mxq(x, axis, fmt="e4m3"):
    dtype, down = {"e4m3": (ml_dtypes.float8_e4m3fn, 7), "e5m2": (ml_dtypes.float8_e5m2, 14)}[fmt]
    v = np.moveaxis(np.asarray(x, np.float32).astype(ml_dtypes.bfloat16).astype(np.float64), axis, -1)
    blocks = v.reshape(v.shape[:-1] + (-1, 32))
    amax = np.abs(blocks).max(-1, keepdims=True)
    byte = np.maximum(np.where(amax > 0, np.frexp(amax)[1] - 1 + 127, 0) - down, 1)
    scale = np.exp2(byte - 127.0)
    codes = (blocks / scale).astype(np.float32).astype(dtype).astype(np.float64)
    return np.moveaxis((codes * scale).reshape(v.shape), -1, axis)


WIDE = False


def mx_kscale(k):
    if not WIDE:
        return np.ones(k)
    levels = np.array([10, -10, 5, -5, 0])
    if k % 512:
        return np.exp2(np.random.permutation(np.resize(levels, k // 32))).repeat(32)
    a = np.empty((k // 512, 16))
    for p in range(k // 512):
        a[p, :8] = np.random.permutation(np.resize(levels, 8))
        for g in range(8):
            far = levels[np.abs(levels - a[p, g]) >= 10]
            a[p, g + 8] = far[np.random.randint(len(far))]
    return np.exp2(a.ravel()).repeat(32)


def f64(x):
    return np.asarray(x).astype(np.float64)


def striped(idx):
    return np.tile(idx.reshape(-1, 16).T, (8, 1)).astype(np.uint16)


def unstriped(offs):
    return offs[:16].T.reshape(-1).astype(np.int64)


def pack_weight(w):
    k, n = w.shape
    w = f64(np.asarray(w, np.float32).astype(ml_dtypes.bfloat16)).reshape(k // 32, 32, n)
    amax = np.abs(w).max(1)
    byte = np.clip(np.where(amax > 0, np.frexp(amax)[1] - 1 + 127 - 7, 1), 1, 254)
    scaled = (w * np.exp2(127.0 - byte)[:, None, :]).reshape(k, n).astype(np.float32)
    words = np.ascontiguousarray(scaled.reshape(k // 512, 128, 4, n).transpose(0, 1, 3, 2)).astype(ml_dtypes.float8_e4m3fn).view(np.uint8)
    return words, np.ascontiguousarray(byte.astype(np.uint8).reshape(k // 512, 16, n))


def unpack_weight(words, scales):
    g, p, n, _ = words.shape
    vals = np.ascontiguousarray(words).view(ml_dtypes.float8_e4m3fn).astype(np.float64) * np.repeat(np.exp2(scales.astype(np.float64) - 127.0), 8, axis=1)[..., None]
    return vals.transpose(0, 1, 3, 2).reshape(g * 512, n)


K, T, S, D, N = 1024, 4096, 1024, 4, 256
P = 2 ** 7


def setup_inputs():
    n = np.random.standard_normal
    s = mx_kscale(K)[:, None]
    packed_xT = pack_weight(n((K, T)) * s)
    return {
        "x_words": packed_xT[0],
        "x_scales": packed_xT[1],
        "w1": (n((K, N)) / np.sqrt(K) / s).astype(np.float32),
        "w2": (n((K, N)) / np.sqrt(K) / s).astype(np.float32),
        "dose": (np.tile(np.random.uniform(0.2, 1.0, S), (P, 1))).astype(np.float32),
        "gf0": (-np.random.uniform(0.5, 2.0, (N, 1))).astype(np.float32),
        "gb0": (-np.random.uniform(0.2, 1.5, (N, 1))).astype(np.float32),
        "offs": striped(np.random.permutation(T)[:S]),
    }


def reference(x_words, x_scales, w1, w2, dose, gf0, gb0, offs):
    xq = unpack_weight(x_words, x_scales)[:, unstriped(offs)]
    y2 = ((mxq(f64(w2), 0, "e4m3").T @ xq)) * f64(dose)[:1]
    gb = y2.reshape(len(y2), -1, D).mean(axis=2) + f64(gb0)
    y1 = ((mxq(f64(w1), 0, "e4m3").T @ xq)) * f64(dose)[:1]
    gf = y1.reshape(len(y1), -1, D).mean(axis=2) + f64(gf0)
    ef = np.exp(gf)
    return np.log(np.exp(gb) * (ef + 1.0) + 1.0) - np.log(ef + 1.0)

@@ -1,0 +1,161 @@
+from contextlib import ExitStack
+
+import concourse.mybir as mybir
+from concourse.masks import make_identity
+
+K, T, S, D, N = 1024, 4096, 1024, 4, 256
+FLOPS = 2 * K * (2 * N) * S
+BYTES = K * T + K * T // 32 + 2 * K * N * 4 + S * 4 + 2 * N * 4 + 128 * (S // 16) * 2 + N * (S // D) * 4
+
+F32 = mybir.dt.float32
+BF16 = mybir.dt.bfloat16
+I32 = mybir.dt.int32
+U32 = mybir.dt.uint32
+U16 = mybir.dt.uint16
+U8 = mybir.dt.uint8
+FP8X4 = mybir.dt.float8_e4m3fn_x4
+ACT = mybir.ActivationFunctionType
+ALU = mybir.AluOpType
+
+P = 128
+PACK = 4
+PASSES = K // (P * PACK)
+HALF = P * D
+HALVES = S // HALF
+M_TILES = N // P
+
+
+def tile_picked_ythermo_logz_p_kernel(tc, x_words, x_scales, w1, w2, dose, gf0, gb0, offs, out):
+    nc = tc.nc
+    with ExitStack() as ctx:
+        keep = ctx.enter_context(tc.tile_pool(name="keep", bufs=1))
+        psum = ctx.enter_context(tc.psum_pool(name="psum", bufs=1))
+
+        offsets = keep.tile([P, S // 16], U16, name="offsets")
+
+        words = [keep.tile([P, T], U32, name=f"words{o}", align_bytes=64) for o in range(PASSES)]
+        scale_rows = keep.tile([P, T], U8, name="scale_rows", align_bytes=64)
+        raw = [keep.tile([P, PASSES, PACK, N], F32, name=f"raw{w}") for w in range(2)]
+
+        def load_words(o):
+            nc.sync.dma_start(out=words[o][:].bitcast(I32), in_=x_words[o].rearrange("p n t -> p (n t)").bitcast(I32))
+
+        def load_weights(w, weights):
+            nc.sync.dma_start(out=raw[w][:], in_=weights.rearrange("(o p j) n -> p o j n", o=PASSES, j=PACK))
+
+        nc.vector.memset(scale_rows[:].bitcast(I32), 0)
+        load_weights(0, w1)
+        for q in range(4):
+            nc.sync.dma_start(
+                out=scale_rows[32 * q : 32 * q + 4 * PASSES, :].bitcast(I32),
+                in_=x_scales[:, 4 * q : 4 * q + 4, :].bitcast(I32),
+            )
+        nc.sync.dma_start(offsets[:], offs)
+        load_weights(1, w2)
+        load_words(0)
+        load_words(1)
+
+        dose_col = keep.tile([P, HALVES, D], F32, name="dose_col")
+        nc.sync.dma_start(out=dose_col[:], in_=dose[0].rearrange("(c p d) -> p c d", c=HALVES, d=D))
+        base = []
+        for name, g0 in (("base_f", gf0), ("base_b", gb0)):
+            col = keep.tile([P, M_TILES], F32, name=name)
+            with nc.allow_non_contiguous_dma(reason="one bias value a partition"):
+                nc.sync.dma_start(out=col[:], in_=g0.rearrange("(t p) o -> p (t o)", p=P))
+            base.append(col)
+        ident = keep.tile([P, P], F32, name="ident")
+        make_identity(nc, ident[:])
+
+        picked = [keep.tile([P, S], U32, name=f"picked{o}", align_bytes=64) for o in range(PASSES)]
+
+        def gather_words(o, c):
+            nc.vector.tensor_copy(
+                out=picked[o][:, c * HALF : (c + 1) * HALF].rearrange("p (d v) -> p v d", d=D),
+                in_=words[o][:].indirect(offsets[:, c * HALF // 16 : (c + 1) * HALF // 16]),
+            )
+
+        picked_scales = keep.tile([P, S], U8, name="picked_scales", align_bytes=64)
+        nc.vector.tensor_copy(out=picked_scales[:], in_=scale_rows[:].indirect(offsets[:]))
+        dealt_scales = keep.tile([P, S], U8, name="dealt_scales", align_bytes=64)
+        nc.vector.tensor_copy(
+            out=dealt_scales[:].rearrange("p (c d v) -> p c d v", c=HALVES, d=D),
+            in_=picked_scales[:].rearrange("p (c v d) -> p c d v", c=HALVES, d=D),
+        )
+
+        w_codes = [keep.tile([P, 2 * N], U32, name=f"w_codes{o}", align_bytes=64) for o in range(PASSES)]
+        w_scales = [keep.tile([P, 2 * N], U8, name=f"w_scales{o}", align_bytes=64) for o in range(PASSES)]
+        for w in range(2):
+            for o in range(PASSES):
+                grouped = keep.tile([P, N, PACK], BF16, name=f"grouped{w}{o}", align_bytes=64)
+                nc.scalar.activation(out=grouped[:], in_=raw[w][:, o, :, :].rearrange("p j n -> p n j"), func=ACT.Copy)
+                nc.vector.quantize_mx(
+                    out=w_codes[o][:, w * N : (w + 1) * N].bitcast(FP8X4),
+                    scales=w_scales[o][:, w * N : (w + 1) * N],
+                    in_=grouped[:].rearrange("p n j -> p (n j)"),
+                )
+
+        products = {(c, d): psum.tile([P, 2 * N], F32, name=f"product{c}{d}", tag=f"bank{c}{d}") for c in range(HALVES) for d in range(D)}
+
+        def multiply(o, c):
+            for d in range(D):
+                cols = slice(c * HALF + d * P, c * HALF + (d + 1) * P)
+                nc.tensor.matmul_mx(
+                    out=products[c, d][:],
+                    lhsT=picked[o][:, cols].bitcast(FP8X4),
+                    lhsT_scale=dealt_scales[4 * o :, cols],
+                    rhs=w_codes[o][:].bitcast(FP8X4),
+                    rhs_scale=w_scales[o][:],
+                    start=(o == 0),
+                    stop=(o == PASSES - 1),
+                )
+
+        for c in range(HALVES):
+            gather_words(0, c)
+        for c in range(HALVES):
+            multiply(0, c)
+        for c in range(HALVES):
+            gather_words(1, c)
+        for c in range(HALVES):
+            multiply(1, c)
+
+        pair_sums = {}
+        for c in range(HALVES):
+            for d in range(2):
+                scaled = keep.tile([P, 2 * N], F32, name=f"scaled{c}{d}")
+                nc.scalar.activation(out=scaled[:], in_=products[c, d][:], func=ACT.Copy, scale=dose_col[:, c, d : d + 1])
+                pair = keep.tile([P, 2 * N], F32, name=f"pair{c}{d}")
+                nc.vector.scalar_tensor_tensor(
+                    out=pair[:], in0=products[c, d + 2][:], scalar=dose_col[:, c, d + 2 : d + 3], in1=scaled[:], op0=ALU.mult, op1=ALU.add
+                )
+                pair_sums[c, d] = pair
+
+        ln_in = [keep.tile([P, 2, S // D], F32, name=f"ln_in{t}") for t in range(M_TILES)]
+        exp_b = [keep.tile([P, S // D], F32, name=f"exp_b{t}") for t in range(M_TILES)]
+        for c in range(HALVES):
+            turned = [psum.tile([P, 2 * N], F32, name=f"turned{c}{r}", tag=f"bank{c}{r}") for r in range(4)]
+            for d in range(2):
+                for r in range(4):
+                    nc.tensor.matmul(
+                        out=turned[r][:, 0:P],
+                        lhsT=pair_sums[c, d][:, r * P : (r + 1) * P],
+                        rhs=ident[:],
+                        is_transpose=True,
+                        start=(d == 0),
+                        stop=(d == 1),
+                    )
+            cols = slice(c * P, (c + 1) * P)
+            for r in range(4):
+                w, t = divmod(r, M_TILES)
+                target = ln_in[t][:, 0, cols] if w == 0 else exp_b[t][:, cols]
+                nc.scalar.activation(out=target, in_=turned[r][:, 0:P], func=ACT.Exp, bias=base[w][:, t : t + 1], scale=1.0 / D)
+
+        for t in range(M_TILES):
+            nc.vector.scalar_tensor_tensor(
+                out=ln_in[t][:, 1, :], in0=ln_in[t][:, 0, :], scalar=1.0, in1=exp_b[t][:], op0=ALU.add, op1=ALU.mult
+            )
+        for t in range(M_TILES):
+            logs = keep.tile([P, 2, S // D], F32, name=f"logs{t}")
+            nc.scalar.activation(out=logs[:], in_=ln_in[t][:], func=ACT.Ln, bias=1.0)
+            result = keep.tile([P, S // D], F32, name=f"result{t}")
+            nc.vector.tensor_tensor(out=result[:], in0=logs[:, 1, :], in1=logs[:, 0, :], op=ALU.subtract)
+            nc.sync.dma_start(out=out[t * P : (t + 1) * P, :], in_=result[:])

@@ -23,6 +23,10 @@ PASSES = K // (P * PACK)
 HALF = P * D
 HALVES = S // HALF
 M_TILES = N // P
+V = S // D
+RUN = 4
+EARLY_COLS = 3 * T // 4
+SCALAR_SHARE = 96
 
 
 def tile_picked_ythermo_logz_p_kernel(tc, x_words, x_scales, w1, w2, dose, gf0, gb0, offs, out):
@@ -32,47 +36,39 @@ def tile_picked_ythermo_logz_p_kernel(tc, x_words, x_scales, w1, w2, dose, gf0, 
         psum = ctx.enter_context(tc.psum_pool(name="psum", bufs=1))
 
         offsets = keep.tile([P, S // 16], U16, name="offsets")
-
         words = [keep.tile([P, T], U32, name=f"words{o}", align_bytes=64) for o in range(PASSES)]
         scale_rows = keep.tile([P, T], U8, name="scale_rows", align_bytes=64)
-        raw = [keep.tile([P, PASSES, PACK, N], F32, name=f"raw{w}") for w in range(2)]
+        raw = {(w, o): keep.tile([P, PACK, N], F32, name=f"raw{w}{o}") for w in range(2) for o in range(PASSES)}
 
-        def load_words(o):
-            nc.sync.dma_start(out=words[o][:].bitcast(I32), in_=x_words[o].rearrange("p n t -> p (n t)").bitcast(I32))
+        def load_words(o, cols):
+            source = x_words[o].rearrange("p n t -> p (n t)").bitcast(I32)
+            nc.sync.dma_start(out=words[o][:, cols].bitcast(I32), in_=source[:, cols])
 
-        def load_weights(w, weights):
-            nc.sync.dma_start(out=raw[w][:], in_=weights.rearrange("(o p j) n -> p o j n", o=PASSES, j=PACK))
+        def load_weights(w, o):
+            rows = (w1, w2)[w][o * P * PACK : (o + 1) * P * PACK, :]
+            nc.sync.dma_start(out=raw[w, o][:], in_=rows.rearrange("(p j) n -> p j n", j=PACK))
 
-        nc.vector.memset(scale_rows[:].bitcast(I32), 0)
-        load_weights(0, w1)
-        for q in range(4):
-            nc.sync.dma_start(
-                out=scale_rows[32 * q : 32 * q + 4 * PASSES, :].bitcast(I32),
-                in_=x_scales[:, 4 * q : 4 * q + 4, :].bitcast(I32),
-            )
+        nc.sync.dma_start(out=scale_rows[0:32, :].bitcast(I32), in_=x_scales.rearrange("o q c -> (o q) c").bitcast(I32))
         nc.sync.dma_start(offsets[:], offs)
-        load_weights(1, w2)
-        load_words(0)
-        load_words(1)
-
+        nc.vector.memset(scale_rows[32:64, :].bitcast(I32), 0)
+        nc.vector.memset(scale_rows[64:128, :].bitcast(I32), 0)
+        load_words(0, slice(0, T))
+        load_words(1, slice(0, EARLY_COLS))
+        load_weights(0, 0)
+        load_words(1, slice(EARLY_COLS, T))
+        load_weights(0, 1)
+        load_weights(1, 0)
+        load_weights(1, 1)
         dose_col = keep.tile([P, HALVES, D], F32, name="dose_col")
-        nc.sync.dma_start(out=dose_col[:], in_=dose[0].rearrange("(c p d) -> p c d", c=HALVES, d=D))
+        nc.scalar.dma_start(out=dose_col[:], in_=dose[0].rearrange("(c p d) -> p c d", c=HALVES, d=D))
         base = []
         for name, g0 in (("base_f", gf0), ("base_b", gb0)):
-            col = keep.tile([P, M_TILES], F32, name=name)
+            col = keep.tile([P, M_TILES], F32, name=name, tag=name)
             with nc.allow_non_contiguous_dma(reason="one bias value a partition"):
-                nc.sync.dma_start(out=col[:], in_=g0.rearrange("(t p) o -> p (t o)", p=P))
+                nc.gpsimd.dma_start(out=col[:], in_=g0.rearrange("(t p) o -> p (t o)", p=P))
             base.append(col)
         ident = keep.tile([P, P], F32, name="ident")
         make_identity(nc, ident[:])
-
-        picked = [keep.tile([P, S], U32, name=f"picked{o}", align_bytes=64) for o in range(PASSES)]
-
-        def gather_words(o, c):
-            nc.vector.tensor_copy(
-                out=picked[o][:, c * HALF : (c + 1) * HALF].rearrange("p (d v) -> p v d", d=D),
-                in_=words[o][:].indirect(offsets[:, c * HALF // 16 : (c + 1) * HALF // 16]),
-            )
 
         picked_scales = keep.tile([P, S], U8, name="picked_scales", align_bytes=64)
         nc.vector.tensor_copy(out=picked_scales[:], in_=scale_rows[:].indirect(offsets[:]))
@@ -82,80 +78,128 @@ def tile_picked_ythermo_logz_p_kernel(tc, x_words, x_scales, w1, w2, dose, gf0, 
             in_=picked_scales[:].rearrange("p (c v d) -> p c d v", c=HALVES, d=D),
         )
 
-        w_codes = [keep.tile([P, 2 * N], U32, name=f"w_codes{o}", align_bytes=64) for o in range(PASSES)]
-        w_scales = [keep.tile([P, 2 * N], U8, name=f"w_scales{o}", align_bytes=64) for o in range(PASSES)]
-        for w in range(2):
-            for o in range(PASSES):
-                grouped = keep.tile([P, N, PACK], BF16, name=f"grouped{w}{o}", align_bytes=64)
-                nc.scalar.activation(out=grouped[:], in_=raw[w][:, o, :, :].rearrange("p j n -> p n j"), func=ACT.Copy)
-                nc.vector.quantize_mx(
-                    out=w_codes[o][:, w * N : (w + 1) * N].bitcast(FP8X4),
-                    scales=w_scales[o][:, w * N : (w + 1) * N],
-                    in_=grouped[:].rearrange("p n j -> p (n j)"),
+        planes = [keep.tile([P, S], U8, name=f"planes{o}", align_bytes=64) for o in range(PASSES)]
+        for o in range(PASSES):
+            nc.vector.memset(planes[o][:].bitcast(I32), 0)
+            for q in range(4):
+                nc.gpsimd.dma_start(
+                    out=planes[o][32 * q + 4 * o : 32 * q + 4 * o + 4, :].bitcast(I32),
+                    in_=dealt_scales[16 * o + 4 * q : 16 * o + 4 * q + 4, :].bitcast(I32),
                 )
+
+        picked = {(o, c): keep.tile([P, HALF], U32, name=f"picked{o}{c}", align_bytes=64) for o in range(PASSES) for c in range(HALVES)}
+
+        def gather_words(o):
+            for c in range(HALVES):
+                nc.vector.tensor_copy(
+                    out=picked[o, c][:].rearrange("p (d v) -> p v d", d=D),
+                    in_=words[o][:].indirect(offsets[:, c * HALF // 16 : (c + 1) * HALF // 16]),
+                )
+
+        w_codes, w_scales = {}, {}
+
+        def quantize_weights(w, o, scalar_cols, tag):
+            grouped = keep.tile([P, N, PACK], BF16, name=f"grouped{w}{o}", tag=tag, align_bytes=64)
+            target = grouped[:].rearrange("p (b i) j -> p b j i", i=RUN)
+            source = raw[w, o][:].rearrange("p j (b i) -> p b j i", i=RUN)
+            cut = scalar_cols // RUN
+            if scalar_cols > 0:
+                nc.scalar.activation(out=target[:, :cut, :, :], in_=source[:, :cut, :, :], func=ACT.Copy)
+            if scalar_cols < N:
+                nc.vector.tensor_copy(out=target[:, cut:, :, :], in_=source[:, cut:, :, :])
+            w_codes[w, o] = keep.tile([P, N], U32, name=f"w_codes{w}{o}", align_bytes=64)
+            w_scales[w, o] = keep.tile([P, N], U8, name=f"w_scales{w}{o}", align_bytes=64)
+            nc.vector.quantize_mx(
+                out=w_codes[w, o][:].bitcast(FP8X4), scales=w_scales[w, o][:], in_=grouped[:].rearrange("p n j -> p (n j)")
+            )
 
         products = {(c, d): psum.tile([P, 2 * N], F32, name=f"product{c}{d}", tag=f"bank{c}{d}") for c in range(HALVES) for d in range(D)}
 
-        def multiply(o, c):
-            for d in range(D):
-                cols = slice(c * HALF + d * P, c * HALF + (d + 1) * P)
+        def multiply(w, o):
+            for c, d in products:
                 nc.tensor.matmul_mx(
-                    out=products[c, d][:],
-                    lhsT=picked[o][:, cols].bitcast(FP8X4),
-                    lhsT_scale=dealt_scales[4 * o :, cols],
-                    rhs=w_codes[o][:].bitcast(FP8X4),
-                    rhs_scale=w_scales[o][:],
+                    out=products[c, d][:, w * N : (w + 1) * N],
+                    lhsT=picked[o, c][:, d * P : (d + 1) * P].bitcast(FP8X4),
+                    lhsT_scale=planes[o][4 * o :, c * HALF + d * P : c * HALF + (d + 1) * P],
+                    rhs=w_codes[w, o][:].bitcast(FP8X4),
+                    rhs_scale=w_scales[w, o][:],
                     start=(o == 0),
                     stop=(o == PASSES - 1),
                 )
 
-        for c in range(HALVES):
-            gather_words(0, c)
-        for c in range(HALVES):
-            multiply(0, c)
-        for c in range(HALVES):
-            gather_words(1, c)
-        for c in range(HALVES):
-            multiply(1, c)
-
         pair_sums = {}
-        for c in range(HALVES):
-            for d in range(2):
-                scaled = keep.tile([P, 2 * N], F32, name=f"scaled{c}{d}")
-                nc.scalar.activation(out=scaled[:], in_=products[c, d][:], func=ACT.Copy, scale=dose_col[:, c, d : d + 1])
-                pair = keep.tile([P, 2 * N], F32, name=f"pair{c}{d}")
-                nc.vector.scalar_tensor_tensor(
-                    out=pair[:], in0=products[c, d + 2][:], scalar=dose_col[:, c, d + 2 : d + 3], in1=scaled[:], op0=ALU.mult, op1=ALU.add
-                )
-                pair_sums[c, d] = pair
 
-        ln_in = [keep.tile([P, 2, S // D], F32, name=f"ln_in{t}") for t in range(M_TILES)]
-        exp_b = [keep.tile([P, S // D], F32, name=f"exp_b{t}") for t in range(M_TILES)]
-        for c in range(HALVES):
-            turned = [psum.tile([P, 2 * N], F32, name=f"turned{c}{r}", tag=f"bank{c}{r}") for r in range(4)]
-            for d in range(2):
-                for r in range(4):
-                    nc.tensor.matmul(
-                        out=turned[r][:, 0:P],
-                        lhsT=pair_sums[c, d][:, r * P : (r + 1) * P],
-                        rhs=ident[:],
-                        is_transpose=True,
-                        start=(d == 0),
-                        stop=(d == 1),
+        def weigh(w):
+            cols = slice(w * N, (w + 1) * N)
+            for c in range(HALVES):
+                for d in range(D // 2):
+                    scaled = keep.tile([P, N], F32, name=f"scaled{w}{c}{d}")
+                    nc.scalar.activation(out=scaled[:], in_=products[c, d][:, cols], func=ACT.Copy, scale=dose_col[:, c, d : d + 1])
+                    pair_sums[w, c, d] = keep.tile([P, N], F32, name=f"pair{w}{c}{d}")
+                    nc.vector.scalar_tensor_tensor(
+                        out=pair_sums[w, c, d][:],
+                        in0=products[c, d + 2][:, cols],
+                        scalar=dose_col[:, c, d + 2 : d + 3],
+                        in1=scaled[:],
+                        op0=ALU.mult,
+                        op1=ALU.add,
                     )
-            cols = slice(c * P, (c + 1) * P)
-            for r in range(4):
-                w, t = divmod(r, M_TILES)
-                target = ln_in[t][:, 0, cols] if w == 0 else exp_b[t][:, cols]
-                nc.scalar.activation(out=target, in_=turned[r][:, 0:P], func=ACT.Exp, bias=base[w][:, t : t + 1], scale=1.0 / D)
 
-        for t in range(M_TILES):
-            nc.vector.scalar_tensor_tensor(
-                out=ln_in[t][:, 1, :], in0=ln_in[t][:, 0, :], scalar=1.0, in1=exp_b[t][:], op0=ALU.add, op1=ALU.mult
+        gather_words(0)
+        quantize_weights(0, 0, 0, "grouped_first")
+        gather_words(1)
+        quantize_weights(0, 1, N, "grouped")
+        quantize_weights(1, 0, SCALAR_SHARE, "grouped")
+        quantize_weights(1, 1, SCALAR_SHARE, "grouped")
+        multiply(0, 0)
+        multiply(0, 1)
+        multiply(1, 0)
+        weigh(0)
+        multiply(1, 1)
+        weigh(1)
+
+        def turn(bank_cols, w, c, d, t):
+            nc.tensor.matmul(
+                out=bank_cols,
+                lhsT=pair_sums[w, c, d][:, t * P : (t + 1) * P],
+                rhs=ident[:],
+                is_transpose=True,
+                start=(d == 0),
+                stop=(d == D // 2 - 1),
             )
+
+        exp_f = keep.tile([P, M_TILES, V], F32, name="exp_f")
+        for t, bank in ((1, "bank00"), (0, "bank01")):
+            turned = psum.tile([P, 2 * N], F32, name=f"turned_f{t}", tag=bank)
+            for c in range(HALVES):
+                for d in range(D // 2):
+                    turn(turned[:, c * P : (c + 1) * P], 0, c, d, t)
+            nc.scalar.activation(out=exp_f[:, t, :], in_=turned[:, 0:V], func=ACT.Exp, bias=base[0][:, t : t + 1], scale=1.0 / D)
+
+        exp_b = [keep.tile([P, V], F32, name=f"exp_b{t}") for t in range(M_TILES)]
+        for c, banks in enumerate((("bank02", "bank03"), ("bank10", "bank11"))):
+            turned = [psum.tile([P, 2 * N], F32, name=f"turned_b{c}{t}", tag=banks[t]) for t in range(M_TILES)]
+            for d in range(D // 2):
+                for t in range(M_TILES):
+                    turn(turned[t][:, 0:P], 1, c, d, t)
+            for t in range(M_TILES):
+                nc.scalar.activation(
+                    out=exp_b[t][:, c * P : (c + 1) * P], in_=turned[t][:, 0:P], func=ACT.Exp, bias=base[1][:, t : t + 1], scale=1.0 / D
+                )
+
+        total = [keep.tile([P, V], F32, name=f"total{t}") for t in range(M_TILES)]
+        plus_one = keep.tile([P, V], F32, name="plus_one")
+        nc.vector.tensor_scalar(out=plus_one[:], in0=exp_f[:, 1, :], scalar1=1.0, scalar2=None, op0=ALU.add)
+        unfolded = keep.tile([P, V], F32, name="unfolded")
+        nc.vector.reciprocal(out=unfolded[:], in_=plus_one[:])
+        nc.vector.scalar_tensor_tensor(out=total[0][:], in0=exp_f[:, 0, :], scalar=1.0, in1=exp_b[0][:], op0=ALU.add, op1=ALU.mult)
+        nc.vector.tensor_tensor(out=total[1][:], in0=unfolded[:], in1=exp_b[1][:], op=ALU.add)
+        log_without = keep.tile([P, V], F32, name="log_without", tag="base_b")
+        nc.scalar.activation(out=log_without[:], in_=exp_f[:, 0, :], func=ACT.Ln, bias=1.0)
+        log_with = keep.tile([P, V], F32, name="log_with")
+        nc.scalar.activation(out=log_with[:], in_=total[0][:], func=ACT.Ln, bias=1.0)
+        result = [keep.tile([P, V], F32, name=f"result{t}") for t in range(M_TILES)]
+        nc.vector.tensor_tensor(out=result[0][:], in0=log_with[:], in1=log_without[:], op=ALU.subtract)
+        nc.scalar.activation(out=result[1][:], in_=total[1][:], func=ACT.Ln)
         for t in range(M_TILES):
-            logs = keep.tile([P, 2, S // D], F32, name=f"logs{t}")
-            nc.scalar.activation(out=logs[:], in_=ln_in[t][:], func=ACT.Ln, bias=1.0)
-            result = keep.tile([P, S // D], F32, name=f"result{t}")
-            nc.vector.tensor_tensor(out=result[:], in0=logs[:, 1, :], in1=logs[:, 0, :], op=ALU.subtract)
-            nc.sync.dma_start(out=out[t * P : (t + 1) * P, :], in_=result[:])
+            nc.sync.dma_start(out=out[t * P : (t + 1) * P, :], in_=result[t][:])

@@ -82,7 +82,7 @@ def tile_picked_ythermo_logz_p_kernel(tc, x_words, x_scales, w1, w2, dose, gf0, 
         for o in range(PASSES):
             nc.vector.memset(planes[o][:].bitcast(I32), 0)
             for q in range(4):
-                nc.gpsimd.dma_start(
+                (nc.scalar, nc.gpsimd)[o].dma_start(
                     out=planes[o][32 * q + 4 * o : 32 * q + 4 * o + 4, :].bitcast(I32),
                     in_=dealt_scales[16 * o + 4 * q : 16 * o + 4 * q + 4, :].bitcast(I32),
                 )
@@ -202,4 +202,4 @@ def tile_picked_ythermo_logz_p_kernel(tc, x_words, x_scales, w1, w2, dose, gf0, 
         nc.vector.tensor_tensor(out=result[0][:], in0=log_with[:], in1=log_without[:], op=ALU.subtract)
         nc.scalar.activation(out=result[1][:], in_=total[1][:], func=ACT.Ln)
         for t in range(M_TILES):
-            nc.sync.dma_start(out=out[t * P : (t + 1) * P, :], in_=result[t][:])
+            (nc.sync, nc.scalar)[t].dma_start(out=out[t * P : (t + 1) * P, :], in_=result[t][:])

from contextlib import ExitStack

import concourse.mybir as mybir
from concourse.masks import make_identity

K, T, S, D, N = 1024, 4096, 1024, 4, 256
FLOPS = 2 * K * (2 * N) * S
BYTES = K * T + K * T // 32 + 2 * K * N * 4 + S * 4 + 2 * N * 4 + 128 * (S // 16) * 2 + N * (S // D) * 4

F32 = mybir.dt.float32
BF16 = mybir.dt.bfloat16
I32 = mybir.dt.int32
U32 = mybir.dt.uint32
U16 = mybir.dt.uint16
U8 = mybir.dt.uint8
FP8X4 = mybir.dt.float8_e4m3fn_x4
ACT = mybir.ActivationFunctionType
ALU = mybir.AluOpType

P = 128
PACK = 4
PASSES = K // (P * PACK)
HALF = P * D
HALVES = S // HALF
M_TILES = N // P
V = S // D
RUN = 4
EARLY_COLS = 3 * T // 4
SCALAR_SHARE = 96


def tile_picked_ythermo_logz_p_kernel(tc, x_words, x_scales, w1, w2, dose, gf0, gb0, offs, out):
    nc = tc.nc
    with ExitStack() as ctx:
        keep = ctx.enter_context(tc.tile_pool(name="keep", bufs=1))
        psum = ctx.enter_context(tc.psum_pool(name="psum", bufs=1))

        offsets = keep.tile([P, S // 16], U16, name="offsets")
        words = [keep.tile([P, T], U32, name=f"words{o}", align_bytes=64) for o in range(PASSES)]
        scale_rows = keep.tile([P, T], U8, name="scale_rows", align_bytes=64)
        raw = {(w, o): keep.tile([P, PACK, N], F32, name=f"raw{w}{o}") for w in range(2) for o in range(PASSES)}

        def load_words(o, cols):
            source = x_words[o].rearrange("p n t -> p (n t)").bitcast(I32)
            nc.sync.dma_start(out=words[o][:, cols].bitcast(I32), in_=source[:, cols])

        def load_weights(w, o):
            rows = (w1, w2)[w][o * P * PACK : (o + 1) * P * PACK, :]
            nc.sync.dma_start(out=raw[w, o][:], in_=rows.rearrange("(p j) n -> p j n", j=PACK))

        nc.sync.dma_start(out=scale_rows[0:32, :].bitcast(I32), in_=x_scales.rearrange("o q c -> (o q) c").bitcast(I32))
        nc.sync.dma_start(offsets[:], offs)
        nc.vector.memset(scale_rows[32:64, :].bitcast(I32), 0)
        nc.vector.memset(scale_rows[64:128, :].bitcast(I32), 0)
        load_words(0, slice(0, T))
        load_words(1, slice(0, EARLY_COLS))
        load_weights(0, 0)
        load_words(1, slice(EARLY_COLS, T))
        load_weights(0, 1)
        load_weights(1, 0)
        load_weights(1, 1)
        dose_col = keep.tile([P, HALVES, D], F32, name="dose_col")
        nc.scalar.dma_start(out=dose_col[:], in_=dose[0].rearrange("(c p d) -> p c d", c=HALVES, d=D))
        base = []
        for name, g0 in (("base_f", gf0), ("base_b", gb0)):
            col = keep.tile([P, M_TILES], F32, name=name, tag=name)
            with nc.allow_non_contiguous_dma(reason="one bias value a partition"):
                nc.gpsimd.dma_start(out=col[:], in_=g0.rearrange("(t p) o -> p (t o)", p=P))
            base.append(col)
        ident = keep.tile([P, P], F32, name="ident")
        make_identity(nc, ident[:])

        picked_scales = keep.tile([P, S], U8, name="picked_scales", align_bytes=64)
        nc.vector.tensor_copy(out=picked_scales[:], in_=scale_rows[:].indirect(offsets[:]))
        dealt_scales = keep.tile([P, S], U8, name="dealt_scales", align_bytes=64)
        nc.vector.tensor_copy(
            out=dealt_scales[:].rearrange("p (c d v) -> p c d v", c=HALVES, d=D),
            in_=picked_scales[:].rearrange("p (c v d) -> p c d v", c=HALVES, d=D),
        )

        planes = [keep.tile([P, S], U8, name=f"planes{o}", align_bytes=64) for o in range(PASSES)]
        for o in range(PASSES):
            nc.vector.memset(planes[o][:].bitcast(I32), 0)
            for q in range(4):
                (nc.scalar, nc.gpsimd)[o].dma_start(
                    out=planes[o][32 * q + 4 * o : 32 * q + 4 * o + 4, :].bitcast(I32),
                    in_=dealt_scales[16 * o + 4 * q : 16 * o + 4 * q + 4, :].bitcast(I32),
                )

        picked = {(o, c): keep.tile([P, HALF], U32, name=f"picked{o}{c}", align_bytes=64) for o in range(PASSES) for c in range(HALVES)}

        def gather_words(o):
            for c in range(HALVES):
                nc.vector.tensor_copy(
                    out=picked[o, c][:].rearrange("p (d v) -> p v d", d=D),
                    in_=words[o][:].indirect(offsets[:, c * HALF // 16 : (c + 1) * HALF // 16]),
                )

        w_codes, w_scales = {}, {}

        def quantize_weights(w, o, scalar_cols, tag):
            grouped = keep.tile([P, N, PACK], BF16, name=f"grouped{w}{o}", tag=tag, align_bytes=64)
            target = grouped[:].rearrange("p (b i) j -> p b j i", i=RUN)
            source = raw[w, o][:].rearrange("p j (b i) -> p b j i", i=RUN)
            cut = scalar_cols // RUN
            if scalar_cols > 0:
                nc.scalar.activation(out=target[:, :cut, :, :], in_=source[:, :cut, :, :], func=ACT.Copy)
            if scalar_cols < N:
                nc.vector.tensor_copy(out=target[:, cut:, :, :], in_=source[:, cut:, :, :])
            w_codes[w, o] = keep.tile([P, N], U32, name=f"w_codes{w}{o}", align_bytes=64)
            w_scales[w, o] = keep.tile([P, N], U8, name=f"w_scales{w}{o}", align_bytes=64)
            nc.vector.quantize_mx(
                out=w_codes[w, o][:].bitcast(FP8X4), scales=w_scales[w, o][:], in_=grouped[:].rearrange("p n j -> p (n j)")
            )

        products = {(c, d): psum.tile([P, 2 * N], F32, name=f"product{c}{d}", tag=f"bank{c}{d}") for c in range(HALVES) for d in range(D)}

        def multiply(w, o):
            for c, d in products:
                nc.tensor.matmul_mx(
                    out=products[c, d][:, w * N : (w + 1) * N],
                    lhsT=picked[o, c][:, d * P : (d + 1) * P].bitcast(FP8X4),
                    lhsT_scale=planes[o][4 * o :, c * HALF + d * P : c * HALF + (d + 1) * P],
                    rhs=w_codes[w, o][:].bitcast(FP8X4),
                    rhs_scale=w_scales[w, o][:],
                    start=(o == 0),
                    stop=(o == PASSES - 1),
                )

        pair_sums = {}

        def weigh(w):
            cols = slice(w * N, (w + 1) * N)
            for c in range(HALVES):
                for d in range(D // 2):
                    scaled = keep.tile([P, N], F32, name=f"scaled{w}{c}{d}")
                    nc.scalar.activation(out=scaled[:], in_=products[c, d][:, cols], func=ACT.Copy, scale=dose_col[:, c, d : d + 1])
                    pair_sums[w, c, d] = keep.tile([P, N], F32, name=f"pair{w}{c}{d}")
                    nc.vector.scalar_tensor_tensor(
                        out=pair_sums[w, c, d][:],
                        in0=products[c, d + 2][:, cols],
                        scalar=dose_col[:, c, d + 2 : d + 3],
                        in1=scaled[:],
                        op0=ALU.mult,
                        op1=ALU.add,
                    )

        gather_words(0)
        quantize_weights(0, 0, 0, "grouped_first")
        gather_words(1)
        quantize_weights(0, 1, N, "grouped")
        quantize_weights(1, 0, SCALAR_SHARE, "grouped")
        quantize_weights(1, 1, SCALAR_SHARE, "grouped")
        multiply(0, 0)
        multiply(0, 1)
        multiply(1, 0)
        weigh(0)
        multiply(1, 1)
        weigh(1)

        def turn(bank_cols, w, c, d, t):
            nc.tensor.matmul(
                out=bank_cols,
                lhsT=pair_sums[w, c, d][:, t * P : (t + 1) * P],
                rhs=ident[:],
                is_transpose=True,
                start=(d == 0),
                stop=(d == D // 2 - 1),
            )

        exp_f = keep.tile([P, M_TILES, V], F32, name="exp_f")
        for t, bank in ((1, "bank00"), (0, "bank01")):
            turned = psum.tile([P, 2 * N], F32, name=f"turned_f{t}", tag=bank)
            for c in range(HALVES):
                for d in range(D // 2):
                    turn(turned[:, c * P : (c + 1) * P], 0, c, d, t)
            nc.scalar.activation(out=exp_f[:, t, :], in_=turned[:, 0:V], func=ACT.Exp, bias=base[0][:, t : t + 1], scale=1.0 / D)

        exp_b = [keep.tile([P, V], F32, name=f"exp_b{t}") for t in range(M_TILES)]
        for c, banks in enumerate((("bank02", "bank03"), ("bank10", "bank11"))):
            turned = [psum.tile([P, 2 * N], F32, name=f"turned_b{c}{t}", tag=banks[t]) for t in range(M_TILES)]
            for d in range(D // 2):
                for t in range(M_TILES):
                    turn(turned[t][:, 0:P], 1, c, d, t)
            for t in range(M_TILES):
                nc.scalar.activation(
                    out=exp_b[t][:, c * P : (c + 1) * P], in_=turned[t][:, 0:P], func=ACT.Exp, bias=base[1][:, t : t + 1], scale=1.0 / D
                )

        total = [keep.tile([P, V], F32, name=f"total{t}") for t in range(M_TILES)]
        plus_one = keep.tile([P, V], F32, name="plus_one")
        nc.vector.tensor_scalar(out=plus_one[:], in0=exp_f[:, 1, :], scalar1=1.0, scalar2=None, op0=ALU.add)
        unfolded = keep.tile([P, V], F32, name="unfolded")
        nc.vector.reciprocal(out=unfolded[:], in_=plus_one[:])
        nc.vector.scalar_tensor_tensor(out=total[0][:], in0=exp_f[:, 0, :], scalar=1.0, in1=exp_b[0][:], op0=ALU.add, op1=ALU.mult)
        nc.vector.tensor_tensor(out=total[1][:], in0=unfolded[:], in1=exp_b[1][:], op=ALU.add)
        log_without = keep.tile([P, V], F32, name="log_without", tag="base_b")
        nc.scalar.activation(out=log_without[:], in_=exp_f[:, 0, :], func=ACT.Ln, bias=1.0)
        log_with = keep.tile([P, V], F32, name="log_with")
        nc.scalar.activation(out=log_with[:], in_=total[0][:], func=ACT.Ln, bias=1.0)
        result = [keep.tile([P, V], F32, name=f"result{t}") for t in range(M_TILES)]
        nc.vector.tensor_tensor(out=result[0][:], in0=log_with[:], in1=log_without[:], op=ALU.subtract)
        nc.scalar.activation(out=result[1][:], in_=total[1][:], func=ACT.Ln)
        for t in range(M_TILES):
            (nc.sync, nc.scalar)[t].dma_start(out=out[t * P : (t + 1) * P, :], in_=result[t][:])
